import numpy as np
import ml_dtypes


def mxq(x, axis, fmt="e4m3"):
    dtype, down = {"e4m3": (ml_dtypes.float8_e4m3fn, 7), "e5m2": (ml_dtypes.float8_e5m2, 14)}[fmt]
    v = np.moveaxis(np.asarray(x, np.float32).astype(ml_dtypes.bfloat16).astype(np.float64), axis, -1)
    blocks = v.reshape(v.shape[:-1] + (-1, 32))
    amax = np.abs(blocks).max(-1, keepdims=True)
    byte = np.maximum(np.where(amax > 0, np.frexp(amax)[1] - 1 + 127, 0) - down, 1)
    scale = np.exp2(byte - 127.0)
    codes = (blocks / scale).astype(np.float32).astype(dtype).astype(np.float64)
    return np.moveaxis((codes * scale).reshape(v.shape), -1, axis)


WIDE = False


def mx_kscale(k):
    if not WIDE:
        return np.ones(k)
    levels = np.array([10, -10, 5, -5, 0])
    if k % 512:
        return np.exp2(np.random.permutation(np.resize(levels, k // 32))).repeat(32)
    a = np.empty((k // 512, 16))
    for p in range(k // 512):
        a[p, :8] = np.random.permutation(np.resize(levels, 8))
        for g in range(8):
            far = levels[np.abs(levels - a[p, g]) >= 10]
            a[p, g + 8] = far[np.random.randint(len(far))]
    return np.exp2(a.ravel()).repeat(32)


def f64(x):
    return np.asarray(x).astype(np.float64)


def striped(idx):
    return np.tile(idx.reshape(-1, 16).T, (8, 1)).astype(np.uint16)


def unstriped(offs):
    return offs[:16].T.reshape(-1).astype(np.int64)


E2M1 = np.array([0.0, 0.5, 1.0, 1.5, 2.0, 3.0, 4.0, 6.0, -0.0, -0.5, -1.0, -1.5, -2.0, -3.0, -4.0, -6.0])


def pack_weight(w, fmt):
    k, n = w.shape
    w = f64(np.asarray(w, np.float32).astype(ml_dtypes.bfloat16)).reshape(k // 32, 32, n)
    amax = np.abs(w).max(1)
    if fmt == "e4m3":
        byte = np.frexp(amax)[1] - 1 + 127 - 7
    else:
        mant, ex = np.frexp(amax / 6.0)
        byte = np.where(mant > 0.5, ex, ex - 1) + 127
    byte = np.clip(np.where(amax > 0, byte, 1), 1, 254)
    scaled = (w * np.exp2(127.0 - byte)[:, None, :]).reshape(k, n).astype(np.float32)
    by_word = np.ascontiguousarray(scaled.reshape(k // 512, 128, 4, n).transpose(0, 1, 3, 2))
    if fmt == "e4m3":
        words = by_word.astype(ml_dtypes.float8_e4m3fn).view(np.uint8)
    else:
        c = by_word.astype(ml_dtypes.float4_e2m1fn).view(np.uint8) & 0xF
        words = (c[..., 0::2] | (c[..., 1::2] << 4)).reshape(k // 512, 128, 2 * n)
    return np.ascontiguousarray(words), np.ascontiguousarray(byte.astype(np.uint8).reshape(k // 512, 16, n))


def unpack_weight(words, scales, fmt):
    g, _, n = scales.shape
    words = np.ascontiguousarray(words).reshape(g, 128, n, -1)
    if fmt == "e4m3":
        vals = words.view(ml_dtypes.float8_e4m3fn).astype(np.float64)
    else:
        nib = np.empty((g, 128, n, 4), np.uint8)
        nib[..., 0::2] = words & 0xF
        nib[..., 1::2] = words >> 4
        vals = E2M1[nib]
    vals = vals * np.repeat(np.exp2(scales.astype(np.float64) - 127.0), 8, axis=1)[..., None]
    return vals.transpose(0, 1, 3, 2).reshape(g * 512, n)


def gelu(v):
    return 0.5 * v * (1.0 + np.tanh(np.sqrt(2.0 / np.pi) * (v + 0.044715 * v**3)))


K, T, S, H, N, K2, T2, P = 1024, 4096, 1024, 1024, 384, 1024, 2048, 512

def setup_inputs():
    n = np.random.standard_normal
    s = mx_kscale(K)[:, None]
    s2 = mx_kscale(K2)[:, None]
    u = mx_kscale(H)[:, None]
    tab_words, tab_scales = pack_weight(n((K, T)) * s, "e4m3")
    tab2_words, tab2_scales = pack_weight(n((K2, T2)) * s2, "e4m3")
    w2_words, w2_scales = pack_weight(0.66 * n((H, N)) / np.sqrt(H) / u, "e2m1")
    wb_words, wb_scales = pack_weight(n((K2, N)) / np.sqrt(K2) / s2, "e4m3")
    return {
        "tab_words": tab_words, "tab_scales": tab_scales,
        "offs": striped(np.random.permutation(T)[:S]),
        "tab2_words": tab2_words, "tab2_scales": tab2_scales,
        "offs2": striped(np.random.permutation(T2)[:P]),
        "pos1": striped(np.random.permutation(S)[:P]),
        "w1": (n((K, H)) / np.sqrt(K) / s * u.T).astype(np.float32),
        "level": (0.6 * n(H) * u[:, 0]).astype(np.float32),
        "w2_words": w2_words, "w2_scales": w2_scales,
        "wb_words": wb_words, "wb_scales": wb_scales,
        "wd": (n((K2, N)) / np.sqrt(K2) / s2).astype(np.float32),
    }

def reference(tab_words, tab_scales, offs, tab2_words, tab2_scales, offs2, pos1,
              w1, level, w2_words, w2_scales, wb_words, wb_scales, wd):
    v = unpack_weight(tab_words, tab_scales, "e4m3")[:, unstriped(offs)]
    v2 = unpack_weight(tab2_words, tab2_scales, "e4m3")[:, unstriped(offs2)]
    w2 = unpack_weight(w2_words, w2_scales, "e2m1")
    wb = unpack_weight(wb_words, wb_scales, "e4m3")
    h = np.maximum(mxq(f64(w1), 0, "e4m3").T @ v, f64(level)[:, None])
    y0 = w2.T @ mxq(h, 0, "e4m3")
    y = y0 + np.sin(y0)
    b = (wb.T @ v2) * (mxq(f64(wd), 0, "e4m3").T @ v2)
    return np.minimum(y[:, unstriped(pos1)], b)

@@ -1,0 +1,331 @@
+import math
+from contextlib import ExitStack
+
+import concourse.mybir as mybir
+
+K, T, S, H, N, K2, T2, PICKS = 1024, 4096, 1024, 1024, 384, 1024, 2048, 512
+FLOPS = 2 * K * H * S + 2 * H * N * S + 2 * 2 * K2 * N * PICKS
+
+F32 = mybir.dt.float32
+BF16 = mybir.dt.bfloat16
+I32 = mybir.dt.int32
+U32 = mybir.dt.uint32
+U16 = mybir.dt.uint16
+U8 = mybir.dt.uint8
+FP8X4 = mybir.dt.float8_e4m3fn_x4
+FP4X4 = mybir.dt.float4_e2m1fn_x4
+ALU = mybir.AluOpType
+ACT = mybir.ActivationFunctionType
+
+P = 128
+PACK = 4
+K_PASS = P * PACK
+PASSES = 2
+BANK = 512
+QUADS = 4
+N_TILES = N // P
+S_TILES = S // P
+
+
+def tile_list_airway_branch_scores_kernel(
+    tc, tab_words, tab_scales, offs, tab2_words, tab2_scales, offs2, pos1,
+    w1, level, w2_words, w2_scales, wb_words, wb_scales, wd, out,
+):
+    nc = tc.nc
+    with ExitStack() as ctx:
+        keep = ctx.enter_context(tc.tile_pool(name="keep", bufs=1))
+        psum = ctx.enter_context(tc.psum_pool(name="psum", bufs=1))
+
+        def sb(name, shape, dtype):
+            return keep.tile(shape, dtype, name=name, align_bytes=64)
+
+        def bank(i, name):
+            return psum.tile([P, BANK], F32, name=name, tag="bank%d" % i)
+
+        def words_view(dram):
+            return dram.rearrange("p t i -> p (t i)").bitcast(I32)
+
+        idx = sb("idx", [P, S // 16], U16)
+        idx2 = sb("idx2", [P, PICKS // 16], U16)
+        p1 = sb("p1", [P, PICKS // 16], U16)
+
+        tab_sc = sb("tab_sc", [P, T], U8)
+        tab2_sc = sb("tab2_sc", [P, T2], U8)
+        wb_sc = sb("wb_sc", [P, N], U8)
+        w2_sc = sb("w2_sc", [P, PASSES * N], U8)
+        nc.vector.memset(tab_sc[:, : T // 2].bitcast(I32), 0)
+        nc.gpsimd.memset(tab_sc[:, T // 2 :].bitcast(I32), 0)
+        nc.gpsimd.memset(tab2_sc[:].bitcast(I32), 0)
+        nc.gpsimd.memset(wb_sc[:].bitcast(I32), 0)
+        nc.gpsimd.memset(w2_sc[:].bitcast(I32), 0)
+
+        def load_packed_scales(queue, tile, dram):
+            for q in range(QUADS):
+                queue.dma_start(
+                    out=tile[32 * q : 32 * q + 4 * PASSES, :].bitcast(I32),
+                    in_=dram[:, 4 * q : 4 * q + 4, :].bitcast(I32),
+                )
+
+        w1_raw = {}
+
+        def load_w1(a, b):
+            w1_raw[a, b] = sb("w1_raw%d%d" % (a, b), [P, PACK, K_PASS], F32)
+            rows = w1[K_PASS * a : K_PASS * (a + 1), K_PASS * b : K_PASS * (b + 1)]
+            nc.sync.dma_start(out=w1_raw[a, b][:], in_=rows.rearrange("(p j) c -> p j c", j=PACK))
+
+        tab = [sb("tab%d" % a, [P, T], I32) for a in range(PASSES)]
+        tab2 = [sb("tab2_%d" % a, [P, T2], I32) for a in range(PASSES)]
+        lev = sb("lev", [P, PASSES, PACK], F32)
+        w2 = sb("w2", [P, PASSES, 2 * N], U8)
+        wb = sb("wb", [P, PASSES, N], I32)
+        wd_raw = [sb("wd_raw%d" % a, [P, PACK, N], F32) for a in range(PASSES)]
+
+        nc.sync.dma_start(idx[:], offs)
+        nc.sync.dma_start(idx2[:], offs2)
+        nc.sync.dma_start(p1[:], pos1)
+        nc.sync.dma_start(out=lev[:], in_=level.rearrange("(b p t) -> p b t", p=P, t=PACK))
+        load_w1(0, 0)
+        load_packed_scales(nc.sync, tab_sc, tab_scales)
+        nc.sync.dma_start(out=tab[0][:], in_=words_view(tab_words[0]))
+        nc.sync.dma_start(out=tab[1][:], in_=words_view(tab_words[1]))
+        load_packed_scales(nc.sync, tab2_sc, tab2_scales)
+        load_w1(1, 0)
+        load_w1(0, 1)
+        load_w1(1, 1)
+        for q in range(QUADS):
+            nc.sync.dma_start(
+                out=w2_sc[32 * q : 32 * q + 4, :].bitcast(I32).rearrange("r (a n) -> r a n", a=PASSES),
+                in_=w2_scales[:, 4 * q : 4 * q + 4, :].bitcast(I32).rearrange("a r n -> r a n"),
+            )
+        nc.sync.dma_start(out=w2[:].bitcast(I32), in_=w2_words.bitcast(I32).rearrange("a p c -> p a c"))
+        for a in range(PASSES):
+            nc.sync.dma_start(out=tab2[a][:], in_=words_view(tab2_words[a]))
+        load_packed_scales(nc.sync, wb_sc, wb_scales)
+        nc.sync.dma_start(out=wb[:], in_=wb_words.rearrange("a p c i -> p a (c i)").bitcast(I32))
+        for a in range(PASSES):
+            rows = wd[K_PASS * a : K_PASS * (a + 1), :]
+            nc.sync.dma_start(out=wd_raw[a][:], in_=rows.rearrange("(p j) c -> p j c", j=PACK))
+
+        w1_bf, w1_codes, w1_sc = {}, {}, {}
+
+        def round_w1(a, b, m_vector):
+            w1_bf[a, b] = sb("w1_bf%d%d" % (a, b), [P, PACK * K_PASS], BF16)
+            dst = w1_bf[a, b][:].rearrange("p (t m j) -> p m j t", t=PACK, j=PACK)
+            src = w1_raw[a, b][:].rearrange("p j (m t) -> p m j t", t=PACK)
+            if m_vector > 0:
+                nc.vector.tensor_copy(out=dst[:, :m_vector], in_=src[:, :m_vector])
+            if m_vector < P:
+                nc.scalar.copy(out=dst[:, m_vector:], in_=src[:, m_vector:])
+
+        def quantize_w1(a, b):
+            w1_codes[a, b] = sb("w1_codes%d%d" % (a, b), [P, K_PASS], U32)
+            w1_sc[a, b] = sb("w1_sc%d%d" % (a, b), [P, K_PASS], U8)
+            nc.vector.quantize_mx(out=w1_codes[a, b][:].bitcast(FP8X4), scales=w1_sc[a, b][:], in_=w1_bf[a, b][:])
+
+        v = [sb("v%d" % a, [P, S], U32) for a in range(PASSES)]
+        v_sc = sb("v_sc", [P, S], U8)
+        v2 = [sb("v2_%d" % a, [P, PICKS], U32) for a in range(PASSES)]
+        v2_sc = sb("v2_sc", [P, PICKS], U8)
+
+        def gather_v(a, lo, hi):
+            nc.vector.tensor_copy(v[a][:, lo:hi], tab[a][:].bitcast(U32).indirect(idx[:, lo // 16 : hi // 16]))
+
+        lev_bf = [sb("lev_bf%d" % b, [P, 2 * P, PACK], BF16) for b in range(PASSES)]
+        for b in range(PASSES):
+            nc.gpsimd.tensor_copy(out=lev_bf[b][:], in_=lev[:, b : b + 1, :].to_broadcast([P, 2 * P, PACK]))
+
+        round_w1(0, 0, 0)
+        nc.vector.tensor_copy(v_sc[:], tab_sc[:].indirect(idx[:]))
+        quantize_w1(0, 0)
+        gather_v(0, 0, S)
+        gather_v(1, 0, S)
+        round_w1(1, 0, 84)
+        quantize_w1(1, 0)
+        nc.vector.tensor_copy(v2_sc[:], tab2_sc[:].indirect(idx2[:]))
+
+        h_bank = {}
+        h_raw = [sb("h_raw%d" % b, [P, S * PACK], BF16) for b in range(PASSES)]
+        h_bf = h_raw
+        h_codes = [sb("h_codes%d" % b, [P, S], U32) for b in range(PASSES)]
+        h_sc = [sb("h_sc%d" % b, [P, S], U8) for b in range(PASSES)]
+
+        def stage1_pass(b, s, a):
+            if a == 0:
+                h_bank[b, s] = bank(s, "h_bank%d%d" % (b, s))
+            cols = slice(P * s, P * (s + 1))
+            for t in range(PACK):
+                m = slice(P * t, P * (t + 1))
+                nc.tensor.matmul_mx(
+                    out=h_bank[b, s][:, m],
+                    lhsT=w1_codes[a, b][:, m].bitcast(FP8X4),
+                    lhsT_scale=w1_sc[a, b][:, m],
+                    rhs=v[a][:, cols].bitcast(FP8X4),
+                    rhs_scale=v_sc[4 * a :, cols],
+                    start=(a == 0 and t == 0),
+                    stop=(a == PASSES - 1 and t == PACK - 1),
+                )
+
+        def evacuate_h(b, s):
+            dst = h_raw[b][:, BANK * s : BANK * (s + 1)].rearrange("p (n t) -> p n t", t=PACK)
+            nc.scalar.copy(out=dst, in_=h_bank[b, s][:].rearrange("p (t n) -> p n t", t=PACK))
+
+        def floor_h(b, u):
+            cols = slice(2 * BANK * u, 2 * BANK * (u + 1))
+            nc.vector.tensor_tensor(
+                out=h_bf[b][:, cols], in0=h_raw[b][:, cols],
+                in1=lev_bf[b][:].rearrange("p n t -> p (n t)"), op=ALU.max,
+            )
+
+        def quantize_h(b, u):
+            cols = slice(2 * P * u, 2 * P * (u + 1))
+            nc.vector.quantize_mx(
+                out=h_codes[b][:, cols].bitcast(FP8X4), scales=h_sc[b][:, cols],
+                in_=h_bf[b][:, 2 * BANK * u : 2 * BANK * (u + 1)],
+            )
+
+        for s in range(S_TILES):
+            stage1_pass(0, s, 0)
+        for s in range(S_TILES):
+            stage1_pass(0, s, 1)
+        for s in range(4):
+            evacuate_h(0, s)
+        round_w1(0, 1, P)
+        floor_h(0, 0)
+        quantize_w1(0, 1)
+        floor_h(0, 1)
+        quantize_h(0, 0)
+        round_w1(1, 1, P // 2)
+        quantize_h(0, 1)
+        quantize_w1(1, 1)
+        for s in range(4, S_TILES):
+            evacuate_h(0, s)
+        for half in range(2):
+            for a in range(PASSES):
+                for s in range(4 * half, 4 * half + 4):
+                    stage1_pass(1, s, a)
+        floor_h(0, 2)
+        floor_h(0, 3)
+        quantize_h(0, 2)
+        quantize_h(0, 3)
+        for s in range(S_TILES):
+            evacuate_h(1, s)
+
+        y0 = [sb("y0_%d" % n, [P, S], F32) for n in range(N_TILES)]
+
+        def stage2(half):
+            cols = slice(BANK * half, BANK * (half + 1))
+            for n in range(N_TILES):
+                acc = bank(N_TILES * half + n, "y_bank%d%d" % (half, n))
+                for b in range(PASSES):
+                    nc.tensor.matmul_mx(
+                        out=acc[:],
+                        lhsT=w2[:, b, 2 * P * n : 2 * P * (n + 1)].bitcast(FP4X4),
+                        lhsT_scale=w2_sc[:, N * b + P * n : N * b + P * (n + 1)],
+                        rhs=h_codes[b][:, cols].bitcast(FP8X4),
+                        rhs_scale=h_sc[b][:, cols],
+                        start=(b == 0),
+                        stop=(b == PASSES - 1),
+                    )
+                nc.scalar.copy(out=y0[n][:, cols], in_=acc[:])
+
+        floor_h(1, 0)
+        nc.vector.tensor_copy(v2[0][:], tab2[0][:].bitcast(U32).indirect(idx2[:]))
+        quantize_h(1, 0)
+        floor_h(1, 1)
+        nc.vector.tensor_copy(v2[1][:], tab2[1][:].bitcast(U32).indirect(idx2[:]))
+        quantize_h(1, 1)
+        stage2(0)
+        floor_h(1, 2)
+        floor_h(1, 3)
+        quantize_h(1, 2)
+        quantize_h(1, 3)
+        stage2(1)
+
+        wd_bf = [sb("wd_bf%d" % a, [P, N * PACK], BF16) for a in range(PASSES)]
+        wd_codes = [sb("wd_codes%d" % a, [P, N], U32) for a in range(PASSES)]
+        wd_sc = [sb("wd_sc%d" % a, [P, N], U8) for a in range(PASSES)]
+
+        def round_wd(a, engine_copy):
+            engine_copy(
+                out=wd_bf[a][:].rearrange("p (c i j) -> p c j i", i=PACK, j=PACK),
+                in_=wd_raw[a][:].rearrange("p j (c i) -> p c j i", i=PACK),
+            )
+
+        picked = [sb("picked%d" % n, [P, PICKS], F32) for n in range(N_TILES)]
+        turns = [sb("turns%d" % n, [P, PICKS], I32) for n in range(N_TILES)]
+        frac = [sb("frac%d" % n, [P, PICKS], F32) for n in range(N_TILES)]
+        sine = [sb("sine%d" % n, [P, PICKS], F32) for n in range(N_TILES)]
+        y = sine
+        first = [sb("first%d" % n, [P, PICKS], F32) for n in range(N_TILES)]
+        branch = first
+        res = frac
+
+        def pick(n):
+            nc.vector.tensor_copy(picked[n][:], y0[n][:].indirect(p1[:]))
+
+        def count_turns(n):
+            nc.vector.tensor_scalar(out=turns[n][:], in0=picked[n][:], scalar1=1.0 / (2.0 * math.pi), scalar2=None, op0=ALU.mult)
+
+        def reduce_and_sine(n):
+            nc.vector.scalar_tensor_tensor(
+                out=frac[n][:], in0=picked[n][:], scalar=1.0 / (2.0 * math.pi), in1=turns[n][:],
+                op0=ALU.mult, op1=ALU.subtract,
+            )
+            nc.scalar.activation(out=sine[n][:], in_=frac[n][:], func=ACT.Sin, scale=2.0 * math.pi)
+
+        def add_sine(n):
+            nc.vector.tensor_tensor(out=y[n][:], in0=picked[n][:], in1=sine[n][:], op=ALU.add)
+
+        def quantize_wd(a):
+            nc.vector.quantize_mx(out=wd_codes[a][:].bitcast(FP8X4), scales=wd_sc[a][:], in_=wd_bf[a][:])
+
+        def branch_first(n):
+            m = slice(P * n, P * (n + 1))
+            acc = bank(6 + n % 2, "b_bank%d" % n)
+            for a in range(PASSES):
+                nc.tensor.matmul_mx(
+                    out=acc[:], lhsT=wb[:, a, m].bitcast(FP8X4), lhsT_scale=wb_sc[4 * a :, m],
+                    rhs=v2[a][:].bitcast(FP8X4), rhs_scale=v2_sc[4 * a :, :],
+                    start=(a == 0), stop=(a == PASSES - 1),
+                )
+            nc.scalar.copy(out=first[n][:], in_=acc[:])
+
+        def branch_second(n):
+            m = slice(P * n, P * (n + 1))
+            acc = bank(n, "d_bank%d" % n)
+            for a in range(PASSES):
+                nc.tensor.matmul_mx(
+                    out=acc[:], lhsT=wd_codes[a][:, m].bitcast(FP8X4), lhsT_scale=wd_sc[a][:, m],
+                    rhs=v2[a][:].bitcast(FP8X4), rhs_scale=v2_sc[4 * a :, :],
+                    start=(a == 0), stop=(a == PASSES - 1),
+                )
+            nc.vector.tensor_tensor(out=branch[n][:], in0=acc[:], in1=first[n][:], op=ALU.mult)
+
+        def finish(n):
+            nc.vector.tensor_tensor(out=res[n][:], in0=y[n][:], in1=branch[n][:], op=ALU.min)
+            nc.sync.dma_start(out=out[P * n : P * (n + 1), :], in_=res[n][:])
+
+        round_wd(0, nc.vector.tensor_copy)
+        round_wd(1, nc.scalar.copy)
+        pick(0)
+        quantize_wd(0)
+        count_turns(0)
+        pick(1)
+        reduce_and_sine(0)
+        count_turns(1)
+        quantize_wd(1)
+        reduce_and_sine(1)
+        for n in range(N_TILES):
+            branch_first(n)
+        pick(2)
+        add_sine(0)
+        count_turns(2)
+        add_sine(1)
+        reduce_and_sine(2)
+        branch_second(0)
+        branch_second(1)
+        finish(0)
+        branch_second(2)
+        finish(1)
+        add_sine(2)
+        finish(2)

@@ -36,8 +36,8 @@ def tile_list_airway_branch_scores_kernel(
         keep = ctx.enter_context(tc.tile_pool(name="keep", bufs=1))
         psum = ctx.enter_context(tc.psum_pool(name="psum", bufs=1))
 
-        def sb(name, shape, dtype):
-            return keep.tile(shape, dtype, name=name, align_bytes=64)
+        def sb(name, shape, dtype, tag=None):
+            return keep.tile(shape, dtype, name=name, tag=tag or name, align_bytes=64)
 
         def bank(i, name):
             return psum.tile([P, BANK], F32, name=name, tag="bank%d" % i)
@@ -51,13 +51,31 @@ def tile_list_airway_branch_scores_kernel(
 
         tab_sc = sb("tab_sc", [P, T], U8)
         tab2_sc = sb("tab2_sc", [P, T2], U8)
-        wb_sc = sb("wb_sc", [P, N], U8)
+        v_sc = sb("v_sc", [P, PASSES * S], U8)
+        v2_sc = sb("v2_sc", [P, PASSES * PICKS], U8)
+        for rows in (slice(32, 64), slice(64, P)):
+            nc.vector.memset(tab_sc[rows, :].bitcast(I32), 0)
+            nc.gpsimd.memset(tab2_sc[rows, :].bitcast(I32), 0)
+        nc.gpsimd.memset(v_sc[:].bitcast(I32), 0)
+        nc.gpsimd.memset(v2_sc[:].bitcast(I32), 0)
         w2_sc = sb("w2_sc", [P, PASSES * N], U8)
-        nc.vector.memset(tab_sc[:, : T // 2].bitcast(I32), 0)
-        nc.gpsimd.memset(tab_sc[:, T // 2 :].bitcast(I32), 0)
-        nc.gpsimd.memset(tab2_sc[:].bitcast(I32), 0)
-        nc.gpsimd.memset(wb_sc[:].bitcast(I32), 0)
+        wb_sc = sb("wb_sc", [P, N], U8)
         nc.gpsimd.memset(w2_sc[:].bitcast(I32), 0)
+        nc.gpsimd.memset(wb_sc[:].bitcast(I32), 0)
+
+        def load_scale_rows(tile, dram):
+            nc.sync.dma_start(out=tile[0:32, :].bitcast(I32), in_=dram.bitcast(I32).rearrange("a j n -> j a n"))
+
+        def gather_scale_rows(name, tile, offsets, count):
+            rows = sb(name, [P, count], U8)
+            nc.vector.tensor_copy(rows[:], tile[:].indirect(offsets[:]))
+            return rows
+
+        def deal_scale_rows(plane, rows):
+            for q in range(QUADS):
+                nc.gpsimd.dma_start(
+                    out=plane[32 * q : 32 * q + 4, :].bitcast(I32), in_=rows[8 * q : 8 * q + 8, :].bitcast(I32)
+                )
 
         def load_packed_scales(queue, tile, dram):
             for q in range(QUADS):
@@ -68,28 +86,39 @@ def tile_list_airway_branch_scores_kernel(
 
         w1_raw = {}
 
-        def load_w1(a, b):
-            w1_raw[a, b] = sb("w1_raw%d%d" % (a, b), [P, PACK, K_PASS], F32)
+        def load_w1(a, b, tag=None):
+            w1_raw[a, b] = sb("w1_raw%d%d" % (a, b), [P, PACK, K_PASS], F32, tag)
             rows = w1[K_PASS * a : K_PASS * (a + 1), K_PASS * b : K_PASS * (b + 1)]
             nc.sync.dma_start(out=w1_raw[a, b][:], in_=rows.rearrange("(p j) c -> p j c", j=PACK))
 
-        tab = [sb("tab%d" % a, [P, T], I32) for a in range(PASSES)]
-        tab2 = [sb("tab2_%d" % a, [P, T2], I32) for a in range(PASSES)]
+        tab = {}
+
+        def load_tab(a, tag):
+            tab[a] = sb("tab%d" % a, [P, T], I32, tag)
+            nc.sync.dma_start(out=tab[a][:], in_=words_view(tab_words[a]))
+
         lev = sb("lev", [P, PASSES, PACK], F32)
-        w2 = sb("w2", [P, PASSES, 2 * N], U8)
-        wb = sb("wb", [P, PASSES, N], I32)
-        wd_raw = [sb("wd_raw%d" % a, [P, PACK, N], F32) for a in range(PASSES)]
+        tab2, wd_raw = {}, {}
+
+        def load_tab2(a, tag):
+            tab2[a] = sb("tab2_%d" % a, [P, T2], I32, tag)
+            nc.sync.dma_start(out=tab2[a][:], in_=words_view(tab2_words[a]))
+
+        def load_wd(a, tag):
+            wd_raw[a] = sb("wd_raw%d" % a, [P, PACK, N], F32, tag)
+            rows = wd[K_PASS * a : K_PASS * (a + 1), :]
+            nc.sync.dma_start(out=wd_raw[a][:], in_=rows.rearrange("(p j) c -> p j c", j=PACK))
 
         nc.sync.dma_start(idx[:], offs)
+        load_scale_rows(tab_sc, tab_scales)
         nc.sync.dma_start(idx2[:], offs2)
-        nc.sync.dma_start(p1[:], pos1)
-        nc.sync.dma_start(out=lev[:], in_=level.rearrange("(b p t) -> p b t", p=P, t=PACK))
+        load_scale_rows(tab2_sc, tab2_scales)
         load_w1(0, 0)
-        load_packed_scales(nc.sync, tab_sc, tab_scales)
-        nc.sync.dma_start(out=tab[0][:], in_=words_view(tab_words[0]))
-        nc.sync.dma_start(out=tab[1][:], in_=words_view(tab_words[1]))
-        load_packed_scales(nc.sync, tab2_sc, tab2_scales)
+        nc.sync.dma_start(out=lev[:], in_=level.rearrange("(b p t) -> p b t", p=P, t=PACK))
+        load_tab(0, None)
         load_w1(1, 0)
+        load_tab(1, None)
+        nc.sync.dma_start(p1[:], pos1)
         load_w1(0, 1)
         load_w1(1, 1)
         for q in range(QUADS):
@@ -97,19 +126,24 @@ def tile_list_airway_branch_scores_kernel(
                 out=w2_sc[32 * q : 32 * q + 4, :].bitcast(I32).rearrange("r (a n) -> r a n", a=PASSES),
                 in_=w2_scales[:, 4 * q : 4 * q + 4, :].bitcast(I32).rearrange("a r n -> r a n"),
             )
+        w2 = sb("w2", [P, PASSES, 2 * N], U8)
         nc.sync.dma_start(out=w2[:].bitcast(I32), in_=w2_words.bitcast(I32).rearrange("a p c -> p a c"))
-        for a in range(PASSES):
-            nc.sync.dma_start(out=tab2[a][:], in_=words_view(tab2_words[a]))
+        load_tab2(0, None)
+        load_tab2(1, None)
         load_packed_scales(nc.sync, wb_sc, wb_scales)
+        wb = sb("wb", [P, PASSES, N], I32)
         nc.sync.dma_start(out=wb[:], in_=wb_words.rearrange("a p c i -> p a (c i)").bitcast(I32))
-        for a in range(PASSES):
-            rows = wd[K_PASS * a : K_PASS * (a + 1), :]
-            nc.sync.dma_start(out=wd_raw[a][:], in_=rows.rearrange("(p j) c -> p j c", j=PACK))
+        load_wd(0, None)
+        load_wd(1, None)
+        v_rows = gather_scale_rows("v_rows", tab_sc, idx, S)
+        deal_scale_rows(v_sc, v_rows)
+        v2_rows = gather_scale_rows("v2_rows", tab2_sc, idx2, PICKS)
+        deal_scale_rows(v2_sc, v2_rows)
 
         w1_bf, w1_codes, w1_sc = {}, {}, {}
 
         def round_w1(a, b, m_vector):
-            w1_bf[a, b] = sb("w1_bf%d%d" % (a, b), [P, PACK * K_PASS], BF16)
+            w1_bf[a, b] = sb("w1_bf%d%d" % (a, b), [P, PACK * K_PASS], BF16, "tab1" if b else None)
             dst = w1_bf[a, b][:].rearrange("p (t m j) -> p m j t", t=PACK, j=PACK)
             src = w1_raw[a, b][:].rearrange("p j (m t) -> p m j t", t=PACK)
             if m_vector > 0:
@@ -122,30 +156,33 @@ def tile_list_airway_branch_scores_kernel(
             w1_sc[a, b] = sb("w1_sc%d%d" % (a, b), [P, K_PASS], U8)
             nc.vector.quantize_mx(out=w1_codes[a, b][:].bitcast(FP8X4), scales=w1_sc[a, b][:], in_=w1_bf[a, b][:])
 
-        v = [sb("v%d" % a, [P, S], U32) for a in range(PASSES)]
-        v_sc = sb("v_sc", [P, S], U8)
-        v2 = [sb("v2_%d" % a, [P, PICKS], U32) for a in range(PASSES)]
-        v2_sc = sb("v2_sc", [P, PICKS], U8)
+        v = {}
+        v2 = {}
+
+        def gather_v2(a, tag):
+            v2[a] = sb("v2_%d" % a, [P, PICKS], U32, tag)
+            nc.vector.tensor_copy(v2[a][:], tab2[a][:].bitcast(U32).indirect(idx2[:]))
+
 
         def gather_v(a, lo, hi):
             nc.vector.tensor_copy(v[a][:, lo:hi], tab[a][:].bitcast(U32).indirect(idx[:, lo // 16 : hi // 16]))
 
-        lev_bf = [sb("lev_bf%d" % b, [P, 2 * P, PACK], BF16) for b in range(PASSES)]
-        for b in range(PASSES):
-            nc.gpsimd.tensor_copy(out=lev_bf[b][:], in_=lev[:, b : b + 1, :].to_broadcast([P, 2 * P, PACK]))
 
         round_w1(0, 0, 0)
-        nc.vector.tensor_copy(v_sc[:], tab_sc[:].indirect(idx[:]))
+        lev_bf = [sb("lev_bf%d" % b, [P, 2 * P, PACK], BF16) for b in range(PASSES)]
+        for b in range(PASSES):
+            nc.scalar.copy(out=lev_bf[b][:], in_=lev[:, b : b + 1, :].to_broadcast([P, 2 * P, PACK]))
         quantize_w1(0, 0)
+        v[0] = sb("v0", [P, S], U32)
         gather_v(0, 0, S)
-        gather_v(1, 0, S)
-        round_w1(1, 0, 84)
+        round_w1(1, 0, 0)
         quantize_w1(1, 0)
-        nc.vector.tensor_copy(v2_sc[:], tab2_sc[:].indirect(idx2[:]))
+        v[1] = sb("v1", [P, S], U32, "w1_bf10")
+        gather_v(1, 0, S // 2)
+        gather_v(1, S // 2, S)
 
         h_bank = {}
         h_raw = [sb("h_raw%d" % b, [P, S * PACK], BF16) for b in range(PASSES)]
-        h_bf = h_raw
         h_codes = [sb("h_codes%d" % b, [P, S], U32) for b in range(PASSES)]
         h_sc = [sb("h_sc%d" % b, [P, S], U8) for b in range(PASSES)]
 
@@ -160,7 +197,7 @@ def tile_list_airway_branch_scores_kernel(
                     lhsT=w1_codes[a, b][:, m].bitcast(FP8X4),
                     lhsT_scale=w1_sc[a, b][:, m],
                     rhs=v[a][:, cols].bitcast(FP8X4),
-                    rhs_scale=v_sc[4 * a :, cols],
+                    rhs_scale=v_sc[:, S * a + P * s : S * a + P * (s + 1)],
                     start=(a == 0 and t == 0),
                     stop=(a == PASSES - 1 and t == PACK - 1),
                 )
@@ -169,18 +206,16 @@ def tile_list_airway_branch_scores_kernel(
             dst = h_raw[b][:, BANK * s : BANK * (s + 1)].rearrange("p (n t) -> p n t", t=PACK)
             nc.scalar.copy(out=dst, in_=h_bank[b, s][:].rearrange("p (t n) -> p n t", t=PACK))
 
-        def floor_h(b, u):
-            cols = slice(2 * BANK * u, 2 * BANK * (u + 1))
-            nc.vector.tensor_tensor(
-                out=h_bf[b][:, cols], in0=h_raw[b][:, cols],
-                in1=lev_bf[b][:].rearrange("p n t -> p (n t)"), op=ALU.max,
-            )
+        def floor_h(b, u, count):
+            part = h_raw[b][:, 2 * BANK * u : 2 * BANK * (u + count)].rearrange("p (u c) -> p u c", u=count)
+            floor = lev_bf[b][:].rearrange("p n t -> p (n t)").unsqueeze(1).to_broadcast([P, count, 2 * BANK])
+            nc.vector.tensor_tensor(out=part, in0=part, in1=floor, op=ALU.max)
 
-        def quantize_h(b, u):
-            cols = slice(2 * P * u, 2 * P * (u + 1))
+        def quantize_h(b, u, count):
+            cols = slice(2 * P * u, 2 * P * (u + count))
             nc.vector.quantize_mx(
                 out=h_codes[b][:, cols].bitcast(FP8X4), scales=h_sc[b][:, cols],
-                in_=h_bf[b][:, 2 * BANK * u : 2 * BANK * (u + 1)],
+                in_=h_raw[b][:, 2 * BANK * u : 2 * BANK * (u + count)],
             )
 
         for s in range(S_TILES):
@@ -190,23 +225,20 @@ def tile_list_airway_branch_scores_kernel(
         for s in range(4):
             evacuate_h(0, s)
         round_w1(0, 1, P)
-        floor_h(0, 0)
         quantize_w1(0, 1)
-        floor_h(0, 1)
-        quantize_h(0, 0)
         round_w1(1, 1, P // 2)
-        quantize_h(0, 1)
+        floor_h(0, 0, 2)
         quantize_w1(1, 1)
+        quantize_h(0, 0, 2)
         for s in range(4, S_TILES):
             evacuate_h(0, s)
         for half in range(2):
             for a in range(PASSES):
                 for s in range(4 * half, 4 * half + 4):
                     stage1_pass(1, s, a)
-        floor_h(0, 2)
-        floor_h(0, 3)
-        quantize_h(0, 2)
-        quantize_h(0, 3)
+        floor_h(0, 2, 2)
+        gather_v2(0, "tab1")
+        quantize_h(0, 2, 2)
         for s in range(S_TILES):
             evacuate_h(1, s)
 
@@ -228,20 +260,17 @@ def tile_list_airway_branch_scores_kernel(
                     )
                 nc.scalar.copy(out=y0[n][:, cols], in_=acc[:])
 
-        floor_h(1, 0)
-        nc.vector.tensor_copy(v2[0][:], tab2[0][:].bitcast(U32).indirect(idx2[:]))
-        quantize_h(1, 0)
-        floor_h(1, 1)
-        nc.vector.tensor_copy(v2[1][:], tab2[1][:].bitcast(U32).indirect(idx2[:]))
-        quantize_h(1, 1)
+        floor_h(1, 0, 2)
+        gather_v2(1, "h_raw0")
+        quantize_h(1, 0, 2)
         stage2(0)
-        floor_h(1, 2)
-        floor_h(1, 3)
-        quantize_h(1, 2)
-        quantize_h(1, 3)
+        floor_h(1, 2, 1)
+        floor_h(1, 3, 1)
+        quantize_h(1, 2, 1)
+        quantize_h(1, 3, 1)
         stage2(1)
 
-        wd_bf = [sb("wd_bf%d" % a, [P, N * PACK], BF16) for a in range(PASSES)]
+        wd_bf = [sb("wd_bf%d" % a, [P, N * PACK], BF16, ("h_raw1", "h_codes1")[a]) for a in range(PASSES)]
         wd_codes = [sb("wd_codes%d" % a, [P, N], U32) for a in range(PASSES)]
         wd_sc = [sb("wd_sc%d" % a, [P, N], U8) for a in range(PASSES)]
 
@@ -281,11 +310,11 @@ def tile_list_airway_branch_scores_kernel(
 
         def branch_first(n):
             m = slice(P * n, P * (n + 1))
-            acc = bank(6 + n % 2, "b_bank%d" % n)
+            acc = bank((6, 7, 3)[n], "b_bank%d" % n)
             for a in range(PASSES):
                 nc.tensor.matmul_mx(
                     out=acc[:], lhsT=wb[:, a, m].bitcast(FP8X4), lhsT_scale=wb_sc[4 * a :, m],
-                    rhs=v2[a][:].bitcast(FP8X4), rhs_scale=v2_sc[4 * a :, :],
+                    rhs=v2[a][:].bitcast(FP8X4), rhs_scale=v2_sc[:, PICKS * a : PICKS * (a + 1)],
                     start=(a == 0), stop=(a == PASSES - 1),
                 )
             nc.scalar.copy(out=first[n][:], in_=acc[:])
@@ -296,7 +325,7 @@ def tile_list_airway_branch_scores_kernel(
             for a in range(PASSES):
                 nc.tensor.matmul_mx(
                     out=acc[:], lhsT=wd_codes[a][:, m].bitcast(FP8X4), lhsT_scale=wd_sc[a][:, m],
-                    rhs=v2[a][:].bitcast(FP8X4), rhs_scale=v2_sc[4 * a :, :],
+                    rhs=v2[a][:].bitcast(FP8X4), rhs_scale=v2_sc[:, PICKS * a : PICKS * (a + 1)],
                     start=(a == 0), stop=(a == PASSES - 1),
                 )
             nc.vector.tensor_tensor(out=branch[n][:], in0=acc[:], in1=first[n][:], op=ALU.mult)

@@ -23,8 +23,13 @@ K_PASS = P * PACK
 PASSES = 2
 BANK = 512
 QUADS = 4
+PLANE_ROWS = 4
+SCALE_ROWS = PASSES * QUADS * PLANE_ROWS
 N_TILES = N // P
 S_TILES = S // P
+HALF = S_TILES // 2
+TURN = 2.0 * math.pi
+WB_BANKS = (6, 7, 3)
 
 
 def tile_list_airway_branch_scores_kernel(
@@ -36,14 +41,11 @@ def tile_list_airway_branch_scores_kernel(
         keep = ctx.enter_context(tc.tile_pool(name="keep", bufs=1))
         psum = ctx.enter_context(tc.psum_pool(name="psum", bufs=1))
 
-        def sb(name, shape, dtype, tag=None):
-            return keep.tile(shape, dtype, name=name, tag=tag or name, align_bytes=64)
+        def sb(name, shape, dtype, reuses=None):
+            return keep.tile(shape, dtype, name=name, tag=reuses or name, align_bytes=64)
 
         def bank(i, name):
             return psum.tile([P, BANK], F32, name=name, tag="bank%d" % i)
-
-        def words_view(dram):
-            return dram.rearrange("p t i -> p (t i)").bitcast(I32)
 
         idx = sb("idx", [P, S // 16], U16)
         idx2 = sb("idx2", [P, PICKS // 16], U16)
@@ -53,7 +55,7 @@ def tile_list_airway_branch_scores_kernel(
         tab2_sc = sb("tab2_sc", [P, T2], U8)
         v_sc = sb("v_sc", [P, PASSES * S], U8)
         v2_sc = sb("v2_sc", [P, PASSES * PICKS], U8)
-        for rows in (slice(32, 64), slice(64, P)):
+        for rows in (slice(SCALE_ROWS, P // 2), slice(P // 2, P)):
             nc.vector.memset(tab_sc[rows, :].bitcast(I32), 0)
             nc.gpsimd.memset(tab2_sc[rows, :].bitcast(I32), 0)
         nc.gpsimd.memset(v_sc[:].bitcast(I32), 0)
@@ -64,88 +66,73 @@ def tile_list_airway_branch_scores_kernel(
         nc.gpsimd.memset(wb_sc[:].bitcast(I32), 0)
 
         def load_scale_rows(tile, dram):
-            nc.sync.dma_start(out=tile[0:32, :].bitcast(I32), in_=dram.bitcast(I32).rearrange("a j n -> j a n"))
+            nc.sync.dma_start(
+                out=tile[0:SCALE_ROWS, :].bitcast(I32), in_=dram.bitcast(I32).rearrange("a g n -> g a n")
+            )
 
-        def gather_scale_rows(name, tile, offsets, count):
-            rows = sb(name, [P, count], U8)
-            nc.vector.tensor_copy(rows[:], tile[:].indirect(offsets[:]))
-            return rows
+        def load_words(name, dram, columns):
+            tile = sb(name, [P, columns], I32)
+            nc.sync.dma_start(out=tile[:], in_=dram.rearrange("p t i -> p (t i)").bitcast(I32))
+            return tile
 
-        def deal_scale_rows(plane, rows):
-            for q in range(QUADS):
-                nc.gpsimd.dma_start(
-                    out=plane[32 * q : 32 * q + 4, :].bitcast(I32), in_=rows[8 * q : 8 * q + 8, :].bitcast(I32)
-                )
+        def load_rows(name, rows, columns):
+            tile = sb(name, [P, PACK, columns], F32)
+            nc.sync.dma_start(out=tile[:], in_=rows.rearrange("(p j) c -> p j c", j=PACK))
+            return tile
 
-        def load_packed_scales(queue, tile, dram):
-            for q in range(QUADS):
-                queue.dma_start(
-                    out=tile[32 * q : 32 * q + 4 * PASSES, :].bitcast(I32),
-                    in_=dram[:, 4 * q : 4 * q + 4, :].bitcast(I32),
-                )
-
-        w1_raw = {}
-
-        def load_w1(a, b, tag=None):
-            w1_raw[a, b] = sb("w1_raw%d%d" % (a, b), [P, PACK, K_PASS], F32, tag)
+        def load_w1(a, b):
             rows = w1[K_PASS * a : K_PASS * (a + 1), K_PASS * b : K_PASS * (b + 1)]
-            nc.sync.dma_start(out=w1_raw[a, b][:], in_=rows.rearrange("(p j) c -> p j c", j=PACK))
+            w1_raw[a, b] = load_rows("w1_raw%d%d" % (a, b), rows, K_PASS)
 
-        tab = {}
-
-        def load_tab(a, tag):
-            tab[a] = sb("tab%d" % a, [P, T], I32, tag)
-            nc.sync.dma_start(out=tab[a][:], in_=words_view(tab_words[a]))
-
+        w1_raw, tab = {}, {}
         lev = sb("lev", [P, PASSES, PACK], F32)
-        tab2, wd_raw = {}, {}
-
-        def load_tab2(a, tag):
-            tab2[a] = sb("tab2_%d" % a, [P, T2], I32, tag)
-            nc.sync.dma_start(out=tab2[a][:], in_=words_view(tab2_words[a]))
-
-        def load_wd(a, tag):
-            wd_raw[a] = sb("wd_raw%d" % a, [P, PACK, N], F32, tag)
-            rows = wd[K_PASS * a : K_PASS * (a + 1), :]
-            nc.sync.dma_start(out=wd_raw[a][:], in_=rows.rearrange("(p j) c -> p j c", j=PACK))
-
         nc.sync.dma_start(idx[:], offs)
         load_scale_rows(tab_sc, tab_scales)
         nc.sync.dma_start(idx2[:], offs2)
         load_scale_rows(tab2_sc, tab2_scales)
         load_w1(0, 0)
         nc.sync.dma_start(out=lev[:], in_=level.rearrange("(b p t) -> p b t", p=P, t=PACK))
-        load_tab(0, None)
+        tab[0] = load_words("tab0", tab_words[0], T)
         load_w1(1, 0)
-        load_tab(1, None)
+        tab[1] = load_words("tab1", tab_words[1], T)
         nc.sync.dma_start(p1[:], pos1)
         load_w1(0, 1)
         load_w1(1, 1)
         for q in range(QUADS):
             nc.sync.dma_start(
-                out=w2_sc[32 * q : 32 * q + 4, :].bitcast(I32).rearrange("r (a n) -> r a n", a=PASSES),
-                in_=w2_scales[:, 4 * q : 4 * q + 4, :].bitcast(I32).rearrange("a r n -> r a n"),
+                out=w2_sc[32 * q : 32 * q + PLANE_ROWS, :].bitcast(I32).rearrange("r (a n) -> r a n", a=PASSES),
+                in_=w2_scales[:, PLANE_ROWS * q : PLANE_ROWS * (q + 1), :].bitcast(I32).rearrange("a r n -> r a n"),
             )
         w2 = sb("w2", [P, PASSES, 2 * N], U8)
         nc.sync.dma_start(out=w2[:].bitcast(I32), in_=w2_words.bitcast(I32).rearrange("a p c -> p a c"))
-        load_tab2(0, None)
-        load_tab2(1, None)
-        load_packed_scales(nc.sync, wb_sc, wb_scales)
+        tab2 = [load_words("tab2_%d" % a, tab2_words[a], T2) for a in range(PASSES)]
+        for q in range(QUADS):
+            nc.sync.dma_start(
+                out=wb_sc[32 * q : 32 * q + PLANE_ROWS * PASSES, :].bitcast(I32),
+                in_=wb_scales[:, PLANE_ROWS * q : PLANE_ROWS * (q + 1), :].bitcast(I32),
+            )
         wb = sb("wb", [P, PASSES, N], I32)
         nc.sync.dma_start(out=wb[:], in_=wb_words.rearrange("a p c i -> p a (c i)").bitcast(I32))
-        load_wd(0, None)
-        load_wd(1, None)
-        v_rows = gather_scale_rows("v_rows", tab_sc, idx, S)
-        deal_scale_rows(v_sc, v_rows)
-        v2_rows = gather_scale_rows("v2_rows", tab2_sc, idx2, PICKS)
-        deal_scale_rows(v2_sc, v2_rows)
+        wd_raw = [load_rows("wd_raw%d" % a, wd[K_PASS * a : K_PASS * (a + 1), :], N) for a in range(PASSES)]
 
-        w1_bf, w1_codes, w1_sc = {}, {}, {}
+        def gather_scales(name, tile, offsets, count, plane):
+            rows = sb(name, [P, count], U8)
+            nc.vector.tensor_copy(rows[:], tile[:].indirect(offsets[:]))
+            for q in range(QUADS):
+                nc.gpsimd.dma_start(
+                    out=plane[32 * q : 32 * q + PLANE_ROWS, :].bitcast(I32),
+                    in_=rows[8 * q : 8 * q + 8, :].bitcast(I32),
+                )
+
+        gather_scales("v_rows", tab_sc, idx, S, v_sc)
+        gather_scales("v2_rows", tab2_sc, idx2, PICKS, v2_sc)
+
+        w1_bf, w1_codes, w1_sc, v, v2 = {}, {}, {}, {}, {}
 
         def round_w1(a, b, m_vector):
             w1_bf[a, b] = sb("w1_bf%d%d" % (a, b), [P, PACK * K_PASS], BF16, "tab1" if b else None)
-            dst = w1_bf[a, b][:].rearrange("p (t m j) -> p m j t", t=PACK, j=PACK)
-            src = w1_raw[a, b][:].rearrange("p j (m t) -> p m j t", t=PACK)
+            dst = w1_bf[a, b][:].rearrange("p (t m j) -> p m t j", t=PACK, j=PACK)
+            src = w1_raw[a, b][:].rearrange("p j (m t) -> p m t j", t=PACK)
             if m_vector > 0:
                 nc.vector.tensor_copy(out=dst[:, :m_vector], in_=src[:, :m_vector])
             if m_vector < P:
@@ -156,22 +143,17 @@ def tile_list_airway_branch_scores_kernel(
             w1_sc[a, b] = sb("w1_sc%d%d" % (a, b), [P, K_PASS], U8)
             nc.vector.quantize_mx(out=w1_codes[a, b][:].bitcast(FP8X4), scales=w1_sc[a, b][:], in_=w1_bf[a, b][:])
 
-        v = {}
-        v2 = {}
-
-        def gather_v2(a, tag):
-            v2[a] = sb("v2_%d" % a, [P, PICKS], U32, tag)
-            nc.vector.tensor_copy(v2[a][:], tab2[a][:].bitcast(U32).indirect(idx2[:]))
-
-
         def gather_v(a, lo, hi):
             nc.vector.tensor_copy(v[a][:, lo:hi], tab[a][:].bitcast(U32).indirect(idx[:, lo // 16 : hi // 16]))
 
+        def gather_v2(a, reuses):
+            v2[a] = sb("v2_%d" % a, [P, PICKS], U32, reuses)
+            nc.vector.tensor_copy(v2[a][:], tab2[a][:].bitcast(U32).indirect(idx2[:]))
 
         round_w1(0, 0, 0)
-        lev_bf = [sb("lev_bf%d" % b, [P, 2 * P, PACK], BF16) for b in range(PASSES)]
+        lev_bf = [sb("lev_bf%d" % b, [P, P, PACK], BF16) for b in range(PASSES)]
         for b in range(PASSES):
-            nc.scalar.copy(out=lev_bf[b][:], in_=lev[:, b : b + 1, :].to_broadcast([P, 2 * P, PACK]))
+            nc.scalar.copy(out=lev_bf[b][:], in_=lev[:, b : b + 1, :].to_broadcast([P, P, PACK]))
         quantize_w1(0, 0)
         v[0] = sb("v0", [P, S], U32)
         gather_v(0, 0, S)
@@ -182,65 +164,63 @@ def tile_list_airway_branch_scores_kernel(
         gather_v(1, S // 2, S)
 
         h_bank = {}
-        h_raw = [sb("h_raw%d" % b, [P, S * PACK], BF16) for b in range(PASSES)]
+        h_bf = [sb("h_bf%d" % b, [P, S * PACK], BF16) for b in range(PASSES)]
         h_codes = [sb("h_codes%d" % b, [P, S], U32) for b in range(PASSES)]
         h_sc = [sb("h_sc%d" % b, [P, S], U8) for b in range(PASSES)]
 
         def stage1_pass(b, s, a):
             if a == 0:
                 h_bank[b, s] = bank(s, "h_bank%d%d" % (b, s))
-            cols = slice(P * s, P * (s + 1))
             for t in range(PACK):
                 m = slice(P * t, P * (t + 1))
                 nc.tensor.matmul_mx(
                     out=h_bank[b, s][:, m],
                     lhsT=w1_codes[a, b][:, m].bitcast(FP8X4),
                     lhsT_scale=w1_sc[a, b][:, m],
-                    rhs=v[a][:, cols].bitcast(FP8X4),
+                    rhs=v[a][:, P * s : P * (s + 1)].bitcast(FP8X4),
                     rhs_scale=v_sc[:, S * a + P * s : S * a + P * (s + 1)],
                     start=(a == 0 and t == 0),
                     stop=(a == PASSES - 1 and t == PACK - 1),
                 )
 
-        def evacuate_h(b, s):
-            dst = h_raw[b][:, BANK * s : BANK * (s + 1)].rearrange("p (n t) -> p n t", t=PACK)
+        def round_h(b, s):
+            dst = h_bf[b][:, BANK * s : BANK * (s + 1)].rearrange("p (n t) -> p n t", t=PACK)
             nc.scalar.copy(out=dst, in_=h_bank[b, s][:].rearrange("p (t n) -> p n t", t=PACK))
 
-        def floor_h(b, u, count):
-            part = h_raw[b][:, 2 * BANK * u : 2 * BANK * (u + count)].rearrange("p (u c) -> p u c", u=count)
-            floor = lev_bf[b][:].rearrange("p n t -> p (n t)").unsqueeze(1).to_broadcast([P, count, 2 * BANK])
+        def floor_h(b, s, count):
+            part = h_bf[b][:, BANK * s : BANK * (s + count)].rearrange("p (u c) -> p u c", u=count)
+            floor = lev_bf[b][:].rearrange("p n t -> p (n t)").unsqueeze(1).to_broadcast([P, count, BANK])
             nc.vector.tensor_tensor(out=part, in0=part, in1=floor, op=ALU.max)
 
-        def quantize_h(b, u, count):
-            cols = slice(2 * P * u, 2 * P * (u + count))
+        def quantize_h(b, s, count):
+            cols = slice(P * s, P * (s + count))
             nc.vector.quantize_mx(
                 out=h_codes[b][:, cols].bitcast(FP8X4), scales=h_sc[b][:, cols],
-                in_=h_raw[b][:, 2 * BANK * u : 2 * BANK * (u + count)],
+                in_=h_bf[b][:, BANK * s : BANK * (s + count)],
             )
 
-        for s in range(S_TILES):
-            stage1_pass(0, s, 0)
-        for s in range(S_TILES):
-            stage1_pass(0, s, 1)
-        for s in range(4):
-            evacuate_h(0, s)
+        for a in range(PASSES):
+            for s in range(S_TILES):
+                stage1_pass(0, s, a)
+        for s in range(HALF):
+            round_h(0, s)
         round_w1(0, 1, P)
         quantize_w1(0, 1)
         round_w1(1, 1, P // 2)
-        floor_h(0, 0, 2)
+        floor_h(0, 0, HALF)
         quantize_w1(1, 1)
-        quantize_h(0, 0, 2)
-        for s in range(4, S_TILES):
-            evacuate_h(0, s)
+        quantize_h(0, 0, HALF)
+        for s in range(HALF, S_TILES):
+            round_h(0, s)
         for half in range(2):
             for a in range(PASSES):
-                for s in range(4 * half, 4 * half + 4):
+                for s in range(HALF * half, HALF * (half + 1)):
                     stage1_pass(1, s, a)
-        floor_h(0, 2, 2)
+        floor_h(0, HALF, HALF)
         gather_v2(0, "tab1")
-        quantize_h(0, 2, 2)
+        quantize_h(0, HALF, HALF)
         for s in range(S_TILES):
-            evacuate_h(1, s)
+            round_h(1, s)
 
         y0 = [sb("y0_%d" % n, [P, S], F32) for n in range(N_TILES)]
 
@@ -260,101 +240,96 @@ def tile_list_airway_branch_scores_kernel(
                     )
                 nc.scalar.copy(out=y0[n][:, cols], in_=acc[:])
 
-        floor_h(1, 0, 2)
-        gather_v2(1, "h_raw0")
-        quantize_h(1, 0, 2)
+        floor_h(1, 0, HALF)
+        quantize_h(1, 0, HALF)
         stage2(0)
-        floor_h(1, 2, 1)
-        floor_h(1, 3, 1)
-        quantize_h(1, 2, 1)
-        quantize_h(1, 3, 1)
+        pairs = (HALF, HALF + 2)
+        for s in pairs:
+            floor_h(1, s, 2)
+        for s in pairs:
+            quantize_h(1, s, 2)
         stage2(1)
+        gather_v2(1, "h_bf1")
 
-        wd_bf = [sb("wd_bf%d" % a, [P, N * PACK], BF16, ("h_raw1", "h_codes1")[a]) for a in range(PASSES)]
+        wd_bf = [sb("wd_bf%d" % a, [P, N * PACK], BF16, ("h_codes1", "h_sc1")[a]) for a in range(PASSES)]
         wd_codes = [sb("wd_codes%d" % a, [P, N], U32) for a in range(PASSES)]
         wd_sc = [sb("wd_sc%d" % a, [P, N], U8) for a in range(PASSES)]
+        picked = [sb("picked%d" % n, [P, PICKS], F32) for n in range(N_TILES)]
+        turns = [sb("turns%d" % n, [P, PICKS], I32) for n in range(N_TILES)]
+        frac = [sb("frac%d" % n, [P, PICKS], F32) for n in range(N_TILES)]
+        y = [sb("y%d" % n, [P, PICKS], F32) for n in range(N_TILES)]
+        branch = [sb("branch%d" % n, [P, PICKS], F32) for n in range(N_TILES)]
 
-        def round_wd(a, engine_copy):
-            engine_copy(
+        def round_wd(a):
+            nc.scalar.copy(
                 out=wd_bf[a][:].rearrange("p (c i j) -> p c j i", i=PACK, j=PACK),
                 in_=wd_raw[a][:].rearrange("p j (c i) -> p c j i", i=PACK),
             )
 
-        picked = [sb("picked%d" % n, [P, PICKS], F32) for n in range(N_TILES)]
-        turns = [sb("turns%d" % n, [P, PICKS], I32) for n in range(N_TILES)]
-        frac = [sb("frac%d" % n, [P, PICKS], F32) for n in range(N_TILES)]
-        sine = [sb("sine%d" % n, [P, PICKS], F32) for n in range(N_TILES)]
-        y = sine
-        first = [sb("first%d" % n, [P, PICKS], F32) for n in range(N_TILES)]
-        branch = first
-        res = frac
+        def quantize_wd(a):
+            nc.vector.quantize_mx(out=wd_codes[a][:].bitcast(FP8X4), scales=wd_sc[a][:], in_=wd_bf[a][:])
 
         def pick(n):
             nc.vector.tensor_copy(picked[n][:], y0[n][:].indirect(p1[:]))
 
         def count_turns(n):
-            nc.vector.tensor_scalar(out=turns[n][:], in0=picked[n][:], scalar1=1.0 / (2.0 * math.pi), scalar2=None, op0=ALU.mult)
+            nc.vector.tensor_scalar(out=turns[n][:], in0=picked[n][:], scalar1=1.0 / TURN, scalar2=None, op0=ALU.mult)
 
-        def reduce_and_sine(n):
+        def sine(n):
             nc.vector.scalar_tensor_tensor(
-                out=frac[n][:], in0=picked[n][:], scalar=1.0 / (2.0 * math.pi), in1=turns[n][:],
+                out=frac[n][:], in0=picked[n][:], scalar=1.0 / TURN, in1=turns[n][:],
                 op0=ALU.mult, op1=ALU.subtract,
             )
-            nc.scalar.activation(out=sine[n][:], in_=frac[n][:], func=ACT.Sin, scale=2.0 * math.pi)
+            nc.scalar.activation(out=y[n][:], in_=frac[n][:], func=ACT.Sin, scale=TURN)
 
         def add_sine(n):
-            nc.vector.tensor_tensor(out=y[n][:], in0=picked[n][:], in1=sine[n][:], op=ALU.add)
+            nc.vector.tensor_tensor(out=y[n][:], in0=picked[n][:], in1=y[n][:], op=ALU.add)
 
-        def quantize_wd(a):
-            nc.vector.quantize_mx(out=wd_codes[a][:].bitcast(FP8X4), scales=wd_sc[a][:], in_=wd_bf[a][:])
-
-        def branch_first(n):
-            m = slice(P * n, P * (n + 1))
-            acc = bank((6, 7, 3)[n], "b_bank%d" % n)
+        def branch_map(acc, codes, scales):
             for a in range(PASSES):
                 nc.tensor.matmul_mx(
-                    out=acc[:], lhsT=wb[:, a, m].bitcast(FP8X4), lhsT_scale=wb_sc[4 * a :, m],
+                    out=acc[:], lhsT=codes[a].bitcast(FP8X4), lhsT_scale=scales[a],
                     rhs=v2[a][:].bitcast(FP8X4), rhs_scale=v2_sc[:, PICKS * a : PICKS * (a + 1)],
                     start=(a == 0), stop=(a == PASSES - 1),
                 )
-            nc.scalar.copy(out=first[n][:], in_=acc[:])
 
-        def branch_second(n):
+        def wb_map(n):
             m = slice(P * n, P * (n + 1))
-            acc = bank(n, "d_bank%d" % n)
-            for a in range(PASSES):
-                nc.tensor.matmul_mx(
-                    out=acc[:], lhsT=wd_codes[a][:, m].bitcast(FP8X4), lhsT_scale=wd_sc[a][:, m],
-                    rhs=v2[a][:].bitcast(FP8X4), rhs_scale=v2_sc[:, PICKS * a : PICKS * (a + 1)],
-                    start=(a == 0), stop=(a == PASSES - 1),
-                )
-            nc.vector.tensor_tensor(out=branch[n][:], in0=acc[:], in1=first[n][:], op=ALU.mult)
+            acc = bank(WB_BANKS[n], "wb_bank%d" % n)
+            branch_map(acc, [wb[:, a, m] for a in range(PASSES)], [wb_sc[PLANE_ROWS * a :, m] for a in range(PASSES)])
+            nc.scalar.copy(out=branch[n][:], in_=acc[:])
+
+        def wd_map_times_wb_map(n):
+            m = slice(P * n, P * (n + 1))
+            acc = bank(n, "wd_bank%d" % n)
+            branch_map(acc, [wd_codes[a][:, m] for a in range(PASSES)], [wd_sc[a][:, m] for a in range(PASSES)])
+            nc.vector.tensor_tensor(out=branch[n][:], in0=acc[:], in1=branch[n][:], op=ALU.mult)
 
         def finish(n):
-            nc.vector.tensor_tensor(out=res[n][:], in0=y[n][:], in1=branch[n][:], op=ALU.min)
-            nc.sync.dma_start(out=out[P * n : P * (n + 1), :], in_=res[n][:])
+            nc.vector.tensor_tensor(out=frac[n][:], in0=y[n][:], in1=branch[n][:], op=ALU.min)
+            nc.sync.dma_start(out=out[P * n : P * (n + 1), :], in_=frac[n][:])
 
-        round_wd(0, nc.vector.tensor_copy)
-        round_wd(1, nc.scalar.copy)
+        round_wd(0)
+        round_wd(1)
         pick(0)
-        quantize_wd(0)
-        count_turns(0)
         pick(1)
-        reduce_and_sine(0)
+        count_turns(0)
         count_turns(1)
-        quantize_wd(1)
-        reduce_and_sine(1)
-        for n in range(N_TILES):
-            branch_first(n)
+        sine(0)
+        sine(1)
         pick(2)
-        add_sine(0)
+        quantize_wd(0)
         count_turns(2)
+        quantize_wd(1)
+        for n in range(N_TILES):
+            wb_map(n)
+        sine(2)
+        add_sine(0)
         add_sine(1)
-        reduce_and_sine(2)
-        branch_second(0)
-        branch_second(1)
-        finish(0)
-        branch_second(2)
-        finish(1)
+        wd_map_times_wb_map(0)
         add_sine(2)
+        wd_map_times_wb_map(1)
+        finish(0)
+        wd_map_times_wb_map(2)
+        finish(1)
         finish(2)

import math
from contextlib import ExitStack

import concourse.mybir as mybir

K, T, S, H, N, K2, T2, PICKS = 1024, 4096, 1024, 1024, 384, 1024, 2048, 512
FLOPS = 2 * K * H * S + 2 * H * N * S + 2 * 2 * K2 * N * PICKS

F32 = mybir.dt.float32
BF16 = mybir.dt.bfloat16
I32 = mybir.dt.int32
U32 = mybir.dt.uint32
U16 = mybir.dt.uint16
U8 = mybir.dt.uint8
FP8X4 = mybir.dt.float8_e4m3fn_x4
FP4X4 = mybir.dt.float4_e2m1fn_x4
ALU = mybir.AluOpType
ACT = mybir.ActivationFunctionType

P = 128
PACK = 4
K_PASS = P * PACK
PASSES = 2
BANK = 512
QUADS = 4
PLANE_ROWS = 4
SCALE_ROWS = PASSES * QUADS * PLANE_ROWS
N_TILES = N // P
S_TILES = S // P
HALF = S_TILES // 2
TURN = 2.0 * math.pi
WB_BANKS = (6, 7, 3)


def tile_list_airway_branch_scores_kernel(
    tc, tab_words, tab_scales, offs, tab2_words, tab2_scales, offs2, pos1,
    w1, level, w2_words, w2_scales, wb_words, wb_scales, wd, out,
):
    nc = tc.nc
    with ExitStack() as ctx:
        keep = ctx.enter_context(tc.tile_pool(name="keep", bufs=1))
        psum = ctx.enter_context(tc.psum_pool(name="psum", bufs=1))

        def sb(name, shape, dtype, reuses=None):
            return keep.tile(shape, dtype, name=name, tag=reuses or name, align_bytes=64)

        def bank(i, name):
            return psum.tile([P, BANK], F32, name=name, tag="bank%d" % i)

        idx = sb("idx", [P, S // 16], U16)
        idx2 = sb("idx2", [P, PICKS // 16], U16)
        p1 = sb("p1", [P, PICKS // 16], U16)

        tab_sc = sb("tab_sc", [P, T], U8)
        tab2_sc = sb("tab2_sc", [P, T2], U8)
        v_sc = sb("v_sc", [P, PASSES * S], U8)
        v2_sc = sb("v2_sc", [P, PASSES * PICKS], U8)
        for rows in (slice(SCALE_ROWS, P // 2), slice(P // 2, P)):
            nc.vector.memset(tab_sc[rows, :].bitcast(I32), 0)
            nc.gpsimd.memset(tab2_sc[rows, :].bitcast(I32), 0)
        nc.gpsimd.memset(v_sc[:].bitcast(I32), 0)
        nc.gpsimd.memset(v2_sc[:].bitcast(I32), 0)
        w2_sc = sb("w2_sc", [P, PASSES * N], U8)
        wb_sc = sb("wb_sc", [P, N], U8)
        nc.gpsimd.memset(w2_sc[:].bitcast(I32), 0)
        nc.gpsimd.memset(wb_sc[:].bitcast(I32), 0)

        def load_scale_rows(tile, dram):
            nc.sync.dma_start(
                out=tile[0:SCALE_ROWS, :].bitcast(I32), in_=dram.bitcast(I32).rearrange("a g n -> g a n")
            )

        def load_words(name, dram, columns):
            tile = sb(name, [P, columns], I32)
            nc.sync.dma_start(out=tile[:], in_=dram.rearrange("p t i -> p (t i)").bitcast(I32))
            return tile

        def load_rows(name, rows, columns):
            tile = sb(name, [P, PACK, columns], F32)
            nc.sync.dma_start(out=tile[:], in_=rows.rearrange("(p j) c -> p j c", j=PACK))
            return tile

        def load_w1(a, b):
            rows = w1[K_PASS * a : K_PASS * (a + 1), K_PASS * b : K_PASS * (b + 1)]
            w1_raw[a, b] = load_rows("w1_raw%d%d" % (a, b), rows, K_PASS)

        w1_raw, tab = {}, {}
        lev = sb("lev", [P, PASSES, PACK], F32)
        nc.sync.dma_start(idx[:], offs)
        load_scale_rows(tab_sc, tab_scales)
        nc.sync.dma_start(idx2[:], offs2)
        load_scale_rows(tab2_sc, tab2_scales)
        load_w1(0, 0)
        nc.sync.dma_start(out=lev[:], in_=level.rearrange("(b p t) -> p b t", p=P, t=PACK))
        tab[0] = load_words("tab0", tab_words[0], T)
        load_w1(1, 0)
        tab[1] = load_words("tab1", tab_words[1], T)
        nc.sync.dma_start(p1[:], pos1)
        load_w1(0, 1)
        load_w1(1, 1)
        for q in range(QUADS):
            nc.sync.dma_start(
                out=w2_sc[32 * q : 32 * q + PLANE_ROWS, :].bitcast(I32).rearrange("r (a n) -> r a n", a=PASSES),
                in_=w2_scales[:, PLANE_ROWS * q : PLANE_ROWS * (q + 1), :].bitcast(I32).rearrange("a r n -> r a n"),
            )
        w2 = sb("w2", [P, PASSES, 2 * N], U8)
        nc.sync.dma_start(out=w2[:].bitcast(I32), in_=w2_words.bitcast(I32).rearrange("a p c -> p a c"))
        tab2 = [load_words("tab2_%d" % a, tab2_words[a], T2) for a in range(PASSES)]
        for q in range(QUADS):
            nc.sync.dma_start(
                out=wb_sc[32 * q : 32 * q + PLANE_ROWS * PASSES, :].bitcast(I32),
                in_=wb_scales[:, PLANE_ROWS * q : PLANE_ROWS * (q + 1), :].bitcast(I32),
            )
        wb = sb("wb", [P, PASSES, N], I32)
        nc.sync.dma_start(out=wb[:], in_=wb_words.rearrange("a p c i -> p a (c i)").bitcast(I32))
        wd_raw = [load_rows("wd_raw%d" % a, wd[K_PASS * a : K_PASS * (a + 1), :], N) for a in range(PASSES)]

        def gather_scales(name, tile, offsets, count, plane):
            rows = sb(name, [P, count], U8)
            nc.vector.tensor_copy(rows[:], tile[:].indirect(offsets[:]))
            for q in range(QUADS):
                nc.gpsimd.dma_start(
                    out=plane[32 * q : 32 * q + PLANE_ROWS, :].bitcast(I32),
                    in_=rows[8 * q : 8 * q + 8, :].bitcast(I32),
                )

        gather_scales("v_rows", tab_sc, idx, S, v_sc)
        gather_scales("v2_rows", tab2_sc, idx2, PICKS, v2_sc)

        w1_bf, w1_codes, w1_sc, v, v2 = {}, {}, {}, {}, {}

        def round_w1(a, b, m_vector):
            w1_bf[a, b] = sb("w1_bf%d%d" % (a, b), [P, PACK * K_PASS], BF16, "tab1" if b else None)
            dst = w1_bf[a, b][:].rearrange("p (t m j) -> p m t j", t=PACK, j=PACK)
            src = w1_raw[a, b][:].rearrange("p j (m t) -> p m t j", t=PACK)
            if m_vector > 0:
                nc.vector.tensor_copy(out=dst[:, :m_vector], in_=src[:, :m_vector])
            if m_vector < P:
                nc.scalar.copy(out=dst[:, m_vector:], in_=src[:, m_vector:])

        def quantize_w1(a, b):
            w1_codes[a, b] = sb("w1_codes%d%d" % (a, b), [P, K_PASS], U32)
            w1_sc[a, b] = sb("w1_sc%d%d" % (a, b), [P, K_PASS], U8)
            nc.vector.quantize_mx(out=w1_codes[a, b][:].bitcast(FP8X4), scales=w1_sc[a, b][:], in_=w1_bf[a, b][:])

        def gather_v(a, lo, hi):
            nc.vector.tensor_copy(v[a][:, lo:hi], tab[a][:].bitcast(U32).indirect(idx[:, lo // 16 : hi // 16]))

        def gather_v2(a, reuses):
            v2[a] = sb("v2_%d" % a, [P, PICKS], U32, reuses)
            nc.vector.tensor_copy(v2[a][:], tab2[a][:].bitcast(U32).indirect(idx2[:]))

        round_w1(0, 0, 0)
        lev_bf = [sb("lev_bf%d" % b, [P, P, PACK], BF16) for b in range(PASSES)]
        for b in range(PASSES):
            nc.scalar.copy(out=lev_bf[b][:], in_=lev[:, b : b + 1, :].to_broadcast([P, P, PACK]))
        quantize_w1(0, 0)
        v[0] = sb("v0", [P, S], U32)
        gather_v(0, 0, S)
        round_w1(1, 0, 0)
        quantize_w1(1, 0)
        v[1] = sb("v1", [P, S], U32, "w1_bf10")
        gather_v(1, 0, S // 2)
        gather_v(1, S // 2, S)

        h_bank = {}
        h_bf = [sb("h_bf%d" % b, [P, S * PACK], BF16) for b in range(PASSES)]
        h_codes = [sb("h_codes%d" % b, [P, S], U32) for b in range(PASSES)]
        h_sc = [sb("h_sc%d" % b, [P, S], U8) for b in range(PASSES)]

        def stage1_pass(b, s, a):
            if a == 0:
                h_bank[b, s] = bank(s, "h_bank%d%d" % (b, s))
            for t in range(PACK):
                m = slice(P * t, P * (t + 1))
                nc.tensor.matmul_mx(
                    out=h_bank[b, s][:, m],
                    lhsT=w1_codes[a, b][:, m].bitcast(FP8X4),
                    lhsT_scale=w1_sc[a, b][:, m],
                    rhs=v[a][:, P * s : P * (s + 1)].bitcast(FP8X4),
                    rhs_scale=v_sc[:, S * a + P * s : S * a + P * (s + 1)],
                    start=(a == 0 and t == 0),
                    stop=(a == PASSES - 1 and t == PACK - 1),
                )

        def round_h(b, s):
            dst = h_bf[b][:, BANK * s : BANK * (s + 1)].rearrange("p (n t) -> p n t", t=PACK)
            nc.scalar.copy(out=dst, in_=h_bank[b, s][:].rearrange("p (t n) -> p n t", t=PACK))

        def floor_h(b, s, count):
            part = h_bf[b][:, BANK * s : BANK * (s + count)].rearrange("p (u c) -> p u c", u=count)
            floor = lev_bf[b][:].rearrange("p n t -> p (n t)").unsqueeze(1).to_broadcast([P, count, BANK])
            nc.vector.tensor_tensor(out=part, in0=part, in1=floor, op=ALU.max)

        def quantize_h(b, s, count):
            cols = slice(P * s, P * (s + count))
            nc.vector.quantize_mx(
                out=h_codes[b][:, cols].bitcast(FP8X4), scales=h_sc[b][:, cols],
                in_=h_bf[b][:, BANK * s : BANK * (s + count)],
            )

        for a in range(PASSES):
            for s in range(S_TILES):
                stage1_pass(0, s, a)
        for s in range(HALF):
            round_h(0, s)
        round_w1(0, 1, P)
        quantize_w1(0, 1)
        round_w1(1, 1, P // 2)
        floor_h(0, 0, HALF)
        quantize_w1(1, 1)
        quantize_h(0, 0, HALF)
        for s in range(HALF, S_TILES):
            round_h(0, s)
        for half in range(2):
            for a in range(PASSES):
                for s in range(HALF * half, HALF * (half + 1)):
                    stage1_pass(1, s, a)
        floor_h(0, HALF, HALF)
        gather_v2(0, "tab1")
        quantize_h(0, HALF, HALF)
        for s in range(S_TILES):
            round_h(1, s)

        y0 = [sb("y0_%d" % n, [P, S], F32) for n in range(N_TILES)]

        def stage2(half):
            cols = slice(BANK * half, BANK * (half + 1))
            for n in range(N_TILES):
                acc = bank(N_TILES * half + n, "y_bank%d%d" % (half, n))
                for b in range(PASSES):
                    nc.tensor.matmul_mx(
                        out=acc[:],
                        lhsT=w2[:, b, 2 * P * n : 2 * P * (n + 1)].bitcast(FP4X4),
                        lhsT_scale=w2_sc[:, N * b + P * n : N * b + P * (n + 1)],
                        rhs=h_codes[b][:, cols].bitcast(FP8X4),
                        rhs_scale=h_sc[b][:, cols],
                        start=(b == 0),
                        stop=(b == PASSES - 1),
                    )
                nc.scalar.copy(out=y0[n][:, cols], in_=acc[:])

        floor_h(1, 0, HALF)
        quantize_h(1, 0, HALF)
        stage2(0)
        pairs = (HALF, HALF + 2)
        for s in pairs:
            floor_h(1, s, 2)
        for s in pairs:
            quantize_h(1, s, 2)
        stage2(1)
        gather_v2(1, "h_bf1")

        wd_bf = [sb("wd_bf%d" % a, [P, N * PACK], BF16, ("h_codes1", "h_sc1")[a]) for a in range(PASSES)]
        wd_codes = [sb("wd_codes%d" % a, [P, N], U32) for a in range(PASSES)]
        wd_sc = [sb("wd_sc%d" % a, [P, N], U8) for a in range(PASSES)]
        picked = [sb("picked%d" % n, [P, PICKS], F32) for n in range(N_TILES)]
        turns = [sb("turns%d" % n, [P, PICKS], I32) for n in range(N_TILES)]
        frac = [sb("frac%d" % n, [P, PICKS], F32) for n in range(N_TILES)]
        y = [sb("y%d" % n, [P, PICKS], F32) for n in range(N_TILES)]
        branch = [sb("branch%d" % n, [P, PICKS], F32) for n in range(N_TILES)]

        def round_wd(a):
            nc.scalar.copy(
                out=wd_bf[a][:].rearrange("p (c i j) -> p c j i", i=PACK, j=PACK),
                in_=wd_raw[a][:].rearrange("p j (c i) -> p c j i", i=PACK),
            )

        def quantize_wd(a):
            nc.vector.quantize_mx(out=wd_codes[a][:].bitcast(FP8X4), scales=wd_sc[a][:], in_=wd_bf[a][:])

        def pick(n):
            nc.vector.tensor_copy(picked[n][:], y0[n][:].indirect(p1[:]))

        def count_turns(n):
            nc.vector.tensor_scalar(out=turns[n][:], in0=picked[n][:], scalar1=1.0 / TURN, scalar2=None, op0=ALU.mult)

        def sine(n):
            nc.vector.scalar_tensor_tensor(
                out=frac[n][:], in0=picked[n][:], scalar=1.0 / TURN, in1=turns[n][:],
                op0=ALU.mult, op1=ALU.subtract,
            )
            nc.scalar.activation(out=y[n][:], in_=frac[n][:], func=ACT.Sin, scale=TURN)

        def add_sine(n):
            nc.vector.tensor_tensor(out=y[n][:], in0=picked[n][:], in1=y[n][:], op=ALU.add)

        def branch_map(acc, codes, scales):
            for a in range(PASSES):
                nc.tensor.matmul_mx(
                    out=acc[:], lhsT=codes[a].bitcast(FP8X4), lhsT_scale=scales[a],
                    rhs=v2[a][:].bitcast(FP8X4), rhs_scale=v2_sc[:, PICKS * a : PICKS * (a + 1)],
                    start=(a == 0), stop=(a == PASSES - 1),
                )

        def wb_map(n):
            m = slice(P * n, P * (n + 1))
            acc = bank(WB_BANKS[n], "wb_bank%d" % n)
            branch_map(acc, [wb[:, a, m] for a in range(PASSES)], [wb_sc[PLANE_ROWS * a :, m] for a in range(PASSES)])
            nc.scalar.copy(out=branch[n][:], in_=acc[:])

        def wd_map_times_wb_map(n):
            m = slice(P * n, P * (n + 1))
            acc = bank(n, "wd_bank%d" % n)
            branch_map(acc, [wd_codes[a][:, m] for a in range(PASSES)], [wd_sc[a][:, m] for a in range(PASSES)])
            nc.vector.tensor_tensor(out=branch[n][:], in0=acc[:], in1=branch[n][:], op=ALU.mult)

        def finish(n):
            nc.vector.tensor_tensor(out=frac[n][:], in0=y[n][:], in1=branch[n][:], op=ALU.min)
            nc.sync.dma_start(out=out[P * n : P * (n + 1), :], in_=frac[n][:])

        round_wd(0)
        round_wd(1)
        pick(0)
        pick(1)
        count_turns(0)
        count_turns(1)
        sine(0)
        sine(1)
        pick(2)
        quantize_wd(0)
        count_turns(2)
        quantize_wd(1)
        for n in range(N_TILES):
            wb_map(n)
        sine(2)
        add_sine(0)
        add_sine(1)
        wd_map_times_wb_map(0)
        add_sine(2)
        wd_map_times_wb_map(1)
        finish(0)
        wd_map_times_wb_map(2)
        finish(1)
        finish(2)
